import numpy as np
import ml_dtypes


def mxq(x, axis, fmt="e4m3"):
    dtype, down = {"e4m3": (ml_dtypes.float8_e4m3fn, 7), "e5m2": (ml_dtypes.float8_e5m2, 14)}[fmt]
    v = np.moveaxis(np.asarray(x, np.float32).astype(ml_dtypes.bfloat16).astype(np.float64), axis, -1)
    blocks = v.reshape(v.shape[:-1] + (-1, 32))
    amax = np.abs(blocks).max(-1, keepdims=True)
    byte = np.maximum(np.where(amax > 0, np.frexp(amax)[1] - 1 + 127, 0) - down, 1)
    scale = np.exp2(byte - 127.0)
    codes = (blocks / scale).astype(np.float32).astype(dtype).astype(np.float64)
    return np.moveaxis((codes * scale).reshape(v.shape), -1, axis)


WIDE = False


def mx_kscale(k):
    if not WIDE:
        return np.ones(k)
    levels = np.array([10, -10, 5, -5, 0])
    if k % 512:
        return np.exp2(np.random.permutation(np.resize(levels, k // 32))).repeat(32)
    a = np.empty((k // 512, 16))
    for p in range(k // 512):
        a[p, :8] = np.random.permutation(np.resize(levels, 8))
        for g in range(8):
            far = levels[np.abs(levels - a[p, g]) >= 10]
            a[p, g + 8] = far[np.random.randint(len(far))]
    return np.exp2(a.ravel()).repeat(32)


def f64(x):
    return np.asarray(x).astype(np.float64)


def striped(idx):
    return np.tile(np.asarray(idx).reshape(-1, 16).T, (8, 1)).astype(np.uint16)


def unstriped(offs):
    return offs[:16].T.reshape(-1).astype(np.int64)


E2M1 = np.array([0.0, 0.5, 1.0, 1.5, 2.0, 3.0, 4.0, 6.0, -0.0, -0.5, -1.0, -1.5, -2.0, -3.0, -4.0, -6.0])


def pack_weight(w, fmt):
    k, n = w.shape
    w = f64(np.asarray(w, np.float32).astype(ml_dtypes.bfloat16)).reshape(k // 32, 32, n)
    amax = np.abs(w).max(1)
    if fmt == "e4m3":
        byte = np.frexp(amax)[1] - 1 + 127 - 7
    else:
        mant, ex = np.frexp(amax / 6.0)
        byte = np.where(mant > 0.5, ex, ex - 1) + 127
    byte = np.clip(np.where(amax > 0, byte, 1), 1, 254)
    scaled = (w * np.exp2(127.0 - byte)[:, None, :]).reshape(k, n).astype(np.float32)
    by_word = np.ascontiguousarray(scaled.reshape(k // 512, 128, 4, n).transpose(0, 1, 3, 2))
    if fmt == "e4m3":
        words = by_word.astype(ml_dtypes.float8_e4m3fn).view(np.uint8)
    else:
        c = by_word.astype(ml_dtypes.float4_e2m1fn).view(np.uint8) & 0xF
        words = (c[..., 0::2] | (c[..., 1::2] << 4)).reshape(k // 512, 128, 2 * n)
    return np.ascontiguousarray(words), np.ascontiguousarray(byte.astype(np.uint8).reshape(k // 512, 16, n))


def unpack_weight(words, scales, fmt):
    g, _, n = scales.shape
    words = np.ascontiguousarray(words).reshape(g, 128, n, -1)
    if fmt == "e4m3":
        vals = words.view(ml_dtypes.float8_e4m3fn).astype(np.float64)
    else:
        nib = np.empty((g, 128, n, 4), np.uint8)
        nib[..., 0::2] = words & 0xF
        nib[..., 1::2] = words >> 4
        vals = E2M1[nib]
    vals = vals * np.repeat(np.exp2(scales.astype(np.float64) - 127.0), 8, axis=1)[..., None]
    return vals.transpose(0, 1, 3, 2).reshape(g * 512, n)


def softplus(v):
    return np.log(1.0 + np.exp(v))


def bf(x):
    return np.asarray(x, np.float32).astype(ml_dtypes.bfloat16)


def planes(Y):
    r, m = Y.shape
    b = f64(bf(Y)).reshape(r // 32, 32, m)
    amax = np.abs(b).max(1)
    byte = np.clip(np.where(amax > 0, np.frexp(amax)[1] - 1 + 127 - 7, 1), 1, 254)
    codes = (b * np.exp2(127.0 - byte)[:, None, :]).reshape(r, m).astype(np.float32).astype(ml_dtypes.float8_e4m3fn).view(np.uint8)
    words = codes.reshape(r // 512, 128, 4, m).transpose(0, 1, 3, 2)
    return np.ascontiguousarray(words), np.ascontiguousarray(byte.astype(np.uint8).reshape(r // 512, 16, m))


K, T, J, N = 1024, 2048, 512, 512


def setup_inputs():
    n = np.random.standard_normal
    idx = np.random.permutation(T)[:J]
    idx2 = np.random.permutation(T)[:J]
    fk = mx_kscale(K)
    wap = pack_weight(n((K, N)) * 1 / np.sqrt(K) * fk[:, None], "e4m3")
    wbp = pack_weight(n((K, N)) * 1 / np.sqrt(K) * fk[:, None], "e2m1")
    return {
        "xt": (n((K, T)) / fk[:, None]).astype(np.float32),
        "wa_words": wap[0],
        "wa_scales": wap[1],
        "wb_words": wbp[0],
        "wb_scales": wbp[1],
        "gm": (np.random.uniform(0.5, 2.0, (N, 1))).astype(np.float32),
        "offs": striped(idx),
        "offs2": striped(idx2),
    }


def reference(xt, wa_words, wa_scales, wb_words, wb_scales, gm, offs, offs2):
    idx = unstriped(offs)
    idx2 = unstriped(offs2)
    wau = unpack_weight(wa_words, wa_scales, "e4m3")
    wbu = unpack_weight(wb_words, wb_scales, "e2m1")
    xtidxq = mxq(f64(xt)[:, idx], 0, "e4m3")
    p = wau.T @ xtidxq
    xtidx2q = mxq(f64(xt)[:, idx2], 0, "e4m3")
    q = wbu.T @ xtidx2q
    y = f64(gm) * softplus(np.abs(p - q))
    words, scales = planes(y)
    return y, words, scales

@@ -1,0 +1,263 @@
+from contextlib import ExitStack
+
+import concourse.mybir as mybir
+
+K, T, J, N = 1024, 2048, 512, 512
+FLOPS = 2 * 2 * K * N * J
+
+F32 = mybir.dt.float32
+BF16 = mybir.dt.bfloat16
+I32 = mybir.dt.int32
+U32 = mybir.dt.uint32
+U16 = mybir.dt.uint16
+U8 = mybir.dt.uint8
+FP8X4 = mybir.dt.float8_e4m3fn_x4
+FP4X4 = mybir.dt.float4_e2m1fn_x4
+ALU = mybir.AluOpType
+ACT = mybir.ActivationFunctionType
+
+P = 128
+PACK = 4
+K_PASS = P * PACK
+HALF = J // 2
+QUARTER = J // 4
+ALIGN = 64
+ARENA_WORDS = 2 * 768 + 2 * 1280 + 2 * N + 2 * 2 * T + 16
+
+CHUNKS = ((0, 768, 768), (768, 1408, 1408), (1408, 2048, 1600))
+THIRD_CHUNKS = ((0, 768, 768), (768, 1408, 1408), (1408, 2048, 1536))
+LAST_CHUNKS = ((0, 768, 768), (768, 1280, 1280), (1280, 1664, 1280), (1664, 2048, 1792))
+VECTOR_BANKS = ((0, 3), (1, 0), (1, 1))
+EXP_RUNS = (((0, 2), (2, 4)), ((2, 4), (0, 1), (1, 2)))
+
+
+def tile_list_gap_of_two_picks_pl_kernel(tc, xt, wa_words, wa_scales, wb_words, wb_scales, gm, offs, offs2, out_0, out_1, out_2):
+    nc = tc.nc
+    with ExitStack() as ctx:
+        keep = ctx.enter_context(tc.tile_pool(name="keep", bufs=1))
+        psum = ctx.enter_context(tc.psum_pool(name="psum", bufs=1))
+        arena = ctx.enter_context(tc.tile_pool(name="arena", bufs=1))
+        places = {}
+        first_free = [2 * 768 * 4]
+
+        def in_arena(name, shape, dtype, nbytes, on=None):
+            if on is None:
+                places[name] = first_free[0]
+                first_free[0] = first_free[0] + (nbytes + ALIGN - 1) // ALIGN * ALIGN
+            return arena.tile(shape, dtype, name=name, tag=name, align_bytes=ALIGN, offset=places[on or name])
+
+        whole = arena.tile([P, ARENA_WORDS], F32, name="whole", align_bytes=ALIGN, offset=0)
+
+        def sb(name, shape, dtype, tag=None):
+            return keep.tile(shape, dtype, name=name, tag=tag or name, align_bytes=ALIGN)
+
+        lists = [keep.tile([P, J // 16], U16, name="first_list"), keep.tile([P, J // 16], U16, name="second_list")]
+        wa_raw = in_arena("wa_raw", [P, 2, N], I32, 8 * N)
+        wb_raw = sb("wb_raw", [P, 2, 2 * N], U8)
+        ws_raw = sb("ws_raw", [P, 2, N], U8)
+        wa = sb("wa", [P, 2, PACK, P], I32)
+        wb = sb("wb", [P, 2, PACK, 2 * P], U8)
+        gain = in_arena("gain", [P, PACK], F32, 16)
+        windows = [sb("window%d" % i, [P, 2 * T], BF16) for i in range(4)]
+        banks = {(h, t): psum.tile([P, HALF], F32, name="bank%d%d" % (h, t)) for h in range(2) for t in range(PACK)}
+
+        nc.gpsimd.memset(ws_raw[:].rearrange("p z n -> p (z n)").bitcast(U32), 0)
+
+        small = [lambda: nc.sync.dma_start(lists[0][:], offs), lambda: nc.sync.dma_start(lists[1][:], offs2)]
+
+        def scale_load(queue, src, row0, quad):
+            dst = ws_raw[32 * quad + row0 : 32 * quad + row0 + 4, :, :].bitcast(I32)
+            queue.dma_start(dst, src[:, 4 * quad : 4 * quad + 4, :].rearrange("z r n -> r z n").bitcast(I32))
+
+        for quad in range(4):
+            scale_load(nc.gpsimd, wb_scales, 0, quad)
+
+        def load_pair(i, chunks, first=0):
+            z, u = divmod(i, 2)
+            rows = xt[z * K_PASS : (z + 1) * K_PASS, :].rearrange("(p u e) c -> p u e c", u=2, e=2)
+            for n, (c0, c1, cut) in list(enumerate(chunks))[first:]:
+                name = "raw%d_%d" % (i, n)
+                if (i, n) == (0, 0):
+                    raw = whole[:, : 2 * (c1 - c0)].rearrange("p (e c) -> p e c", e=2)
+                elif (i, n) <= (1, 0):
+                    raw = sb(name, [P, 2, c1 - c0], F32)[:]
+                else:
+                    raw = in_arena(name, [P, 2, c1 - c0], F32, 8 * (c1 - c0))[:]
+                nc.sync.dma_start(raw, rows[:, u, :, c0:c1])
+                if (i, n) == (1, 0):
+                    for quad in range(4):
+                        scale_load(nc.sync, wa_scales, 4, quad)
+                if (i, n) == (2, 0):
+                    nc.sync.dma_start(wa_raw[:], wa_words.rearrange("z p n r -> p z (n r)").bitcast(I32))
+                if (i, n) == (2, 1):
+                    nc.sync.dma_start(gain[:], gm.rearrange("(p t) o -> p (t o)", t=PACK))
+                if i + n >= 1:
+                    for job in small[:2]:
+                        job()
+                    small[:2] = []
+                dst = windows[i][:].rearrange("p (c e) -> p c e", e=2)
+                src = raw.rearrange("p e c -> p c e")
+                if cut > c0:
+                    nc.scalar.activation(dst[:, c0:cut, :], src[:, : cut - c0, :], ACT.Copy)
+                if cut < c1:
+                    nc.vector.tensor_copy(dst[:, cut:c1, :], src[:, cut - c0 :, :])
+
+        def gather(picked, i, which, j0, j1):
+            window = windows[i][:].bitcast(U32)
+            nc.vector.tensor_copy(picked[:, i % 2, :], window.indirect(lists[which][:, j0 // 16 : j1 // 16]))
+
+        def weave(picked, which, name, width, on_scalar, tag=None, on=None):
+            woven = in_arena(name, [P, PACK * width], BF16, 0, on) if on else sb(name, [P, PACK * width], BF16, tag)
+            if which == 0 and on_scalar:
+                dst = woven[:].bitcast(U32).rearrange("p (j u) -> p j u", u=2)
+                nc.scalar.copy(dst, picked[:].rearrange("p u j -> p j u"))
+            elif which == 0:
+                dst = woven[:].bitcast(I32).rearrange("p (j u) -> p j u", u=2)
+                nc.vector.tensor_copy(dst, picked[:].bitcast(I32).rearrange("p u j -> p j u"))
+            else:
+                dst = woven[:].rearrange("p (j u e) -> p j u e", u=2, e=2)
+                src = picked[:].bitcast(BF16).rearrange("p u (j e) -> p j u e", e=2)
+                if on_scalar:
+                    nc.scalar.activation(dst, src, ACT.Copy, scale=-1.0)
+                else:
+                    nc.vector.tensor_scalar(dst, src, -1.0, None, ALU.mult)
+            return woven
+
+        def quantise(woven, name, width, on=None):
+            codes = in_arena(name + "_codes", [P, width], U32, 0, on) if on else sb(name + "_codes", [P, width], U32)
+            scales = sb(name + "_scales", [P, width], U8)
+            nc.vector.quantize_mx(out=codes[:].bitcast(FP8X4), scales=scales[:], in_=woven[:])
+            return codes, scales
+
+        def multiply(h, t, z, which, operand, j0, start=False, stop=False):
+            codes, scales = operand
+            if which == 0:
+                nc.tensor.matmul_mx(
+                    out=banks[h, t][:], lhsT=wa[:, z, t, :].bitcast(FP8X4), lhsT_scale=ws[4:P, z, t, :],
+                    rhs=codes[:, j0 : j0 + HALF].bitcast(FP8X4), rhs_scale=scales[:, j0 : j0 + HALF],
+                    start=start, stop=stop)
+            else:
+                for s in range(2):
+                    cols = slice(j0 + s * QUARTER, j0 + (s + 1) * QUARTER)
+                    nc.tensor.matmul_mx(
+                        out=banks[h, t][:, s * QUARTER : (s + 1) * QUARTER], lhsT=wb[:, z, t, :].bitcast(FP4X4),
+                        lhsT_scale=ws[:, z, t, :], rhs=codes[:, cols].bitcast(FP8X4), rhs_scale=scales[:, cols],
+                        start=False, stop=stop and s == 1)
+
+        ws = sb("ws", [P, 2, PACK, P], U8, "wb_raw")
+
+
+        picked0 = [sb("picked0_%d" % w, [P, 2, J], U32) for w in range(2)]
+        load_pair(0, CHUNKS)
+        nc.sync.dma_start(wb_raw[:].bitcast(I32), wb_words.rearrange("z p c -> p z c").bitcast(I32))
+        for w in range(2):
+            gather(picked0[w], 0, w, 0, J)
+        nc.vector.tensor_copy(wb[:].bitcast(U16), wb_raw[:].bitcast(U16).rearrange("p z (m t) -> p z t m", t=PACK))
+        load_pair(1, CHUNKS)
+        nc.vector.tensor_copy(ws[:], ws_raw[:].rearrange("p z (m t) -> p z t m", t=PACK))
+        for w in range(2):
+            gather(picked0[w], 1, w, 0, J)
+        pass0 = {1: quantise(weave(picked0[1], 1, "woven0_1", J, False), "x0_1", J)}
+
+        picked1 = {(w, h): sb("picked1_%d%d" % (w, h), [P, 2, HALF], U32) for w in range(2) for h in range(2)}
+        load_pair(2, THIRD_CHUNKS[:1])
+        woven00 = weave(picked0[0], 0, "woven0_0", J, True, on="raw2_0")
+        load_pair(2, THIRD_CHUNKS, 1)
+        nc.vector.tensor_copy(wa[:], wa_raw[:].rearrange("p z (m t) -> p z t m", t=PACK))
+        for h in range(2):
+            for w in range(2):
+                gather(picked1[w, h], 2, w, h * HALF, (h + 1) * HALF)
+        pass0[0] = quantise(woven00, "x0_0", J, on="raw2_2")
+        load_pair(3, LAST_CHUNKS)
+        for h in range(2):
+            for t in range(PACK):
+                multiply(h, t, 0, 0, pass0[0], h * HALF, start=True)
+                multiply(h, t, 0, 1, pass0[1], h * HALF)
+
+        woven1 = {}
+        operands = {}
+        gather(picked1[0, 0], 3, 0, 0, HALF)
+        woven1[0, 0] = weave(picked1[0, 0], 0, "woven1_00", HALF, True)
+        gather(picked1[1, 0], 3, 1, 0, HALF)
+        woven1[1, 0] = weave(picked1[1, 0], 1, "woven1_10", HALF, True)
+        gather(picked1[1, 1], 3, 1, HALF, J)
+        woven1[1, 1] = weave(picked1[1, 1], 1, "woven1_11", HALF, True)
+        gather(picked1[0, 1], 3, 0, HALF, J)
+        operands[0, 0] = quantise(woven1[0, 0], "x1_00", HALF)
+        operands[1, 0] = quantise(woven1[1, 0], "x1_10", HALF)
+        woven1[0, 1] = weave(picked1[0, 1], 0, "woven1_01", HALF, False, tag="woven1_10")
+        operands[1, 1] = quantise(woven1[1, 1], "x1_11", HALF)
+        operands[0, 1] = quantise(woven1[0, 1], "x1_01", HALF)
+
+        gap = sb("gap", [P, 2, PACK, HALF], F32)
+        decay = sb("decay", [P, 2, PACK, HALF], F32)
+        for h in range(2):
+            for t in range(PACK):
+                multiply(h, t, 1, 0, operands[0, h], 0)
+            for t in range(PACK):
+                multiply(h, t, 1, 1, operands[1, h], 0, stop=True)
+            for t in range(PACK):
+                if (h, t) in VECTOR_BANKS:
+                    twice = sb("twice%d%d" % (h, t), [P, HALF], F32)
+                    nc.vector.tensor_scalar(twice[:], banks[h, t][:], 0.0, 2.0, ALU.max, ALU.mult)
+                    nc.vector.scalar_tensor_tensor(gap[:, h, t, :], banks[h, t][:], -1.0, twice[:], ALU.mult, ALU.add)
+                else:
+                    nc.scalar.activation(gap[:, h, t, :], banks[h, t][:], ACT.Abs)
+            for t0, t1 in EXP_RUNS[h]:
+                nc.scalar.activation(decay[:, h, t0:t1, :], gap[:, h, t0:t1, :], ACT.Exp, scale=-1.0)
+        scaled = sb("scaled", [P, 2, PACK, HALF], F32, tag="twice11")
+        for h in range(2):
+            for t in range(PACK):
+                nc.vector.tensor_scalar(scaled[:, h, t, :], gap[:, h, t, :], gain[:, t : t + 1], None, ALU.mult)
+
+        rest = sb("rest", [P, 4, PACK, QUARTER], F32, tag="gap")
+        for c in range(4):
+            h, s = divmod(c, 2)
+            nc.scalar.activation(rest[:, c, :, :], decay[:, h, :, s * QUARTER : (s + 1) * QUARTER], ACT.Ln, bias=1.0)
+
+        y_rows = out_0.rearrange("(p t) j -> p t j", t=PACK)
+        words_out = out_1[0].rearrange("p j r -> p (j r)").bitcast(I32)
+        y_codes = sb("y_codes", [P, J], U32)
+        y_scales = sb("y_scales", [P, J], U8)
+        ys = [sb("y%d" % h, [P, PACK, HALF], F32) for h in range(2)]
+        rounded = [sb("rounded%d" % c, [P, PACK * QUARTER], BF16) for c in range(4)]
+
+        def finish(c):
+            h, s = divmod(c, 2)
+            cols = slice(s * QUARTER, (s + 1) * QUARTER)
+            for t in range(PACK):
+                nc.vector.scalar_tensor_tensor(ys[h][:, t, cols], rest[:, c, t, :], gain[:, t : t + 1], scaled[:, h, t, cols], ALU.mult, ALU.add)
+
+        def round_off(c, on_scalar):
+            h, s = divmod(c, 2)
+            dst = rounded[c][:].rearrange("p (b i t) -> p b t i", i=4, t=PACK)
+            src = ys[h][:, :, s * QUARTER : (s + 1) * QUARTER].rearrange("p t (b i) -> p b t i", i=4)
+            if on_scalar:
+                nc.scalar.activation(dst, src, ACT.Copy)
+            else:
+                nc.vector.tensor_copy(dst, src)
+
+        def planes(c):
+            cols = slice(c * QUARTER, (c + 1) * QUARTER)
+            nc.vector.quantize_mx(out=y_codes[:, cols].bitcast(FP8X4), scales=y_scales[:, cols], in_=rounded[c][:])
+
+        finish(0)
+        finish(1)
+        nc.sync.dma_start(y_rows[:, :, 0:HALF], ys[0][:])
+        round_off(0, True)
+        round_off(1, True)
+        finish(2)
+        nc.sync.dma_start(y_rows[:, :, HALF : HALF + QUARTER], ys[1][:, :, 0:QUARTER])
+        finish(3)
+        nc.sync.dma_start(y_rows[:, :, HALF + QUARTER : J], ys[1][:, :, QUARTER:HALF])
+        round_off(2, False)
+        round_off(3, False)
+        planes(0)
+        planes(1)
+        nc.sync.dma_start(words_out[:, 0:HALF], y_codes[:, 0:HALF].bitcast(I32))
+        planes(2)
+        planes(3)
+        nc.sync.dma_start(words_out[:, HALF:J], y_codes[:, HALF:J].bitcast(I32))
+        for quad in range(4):
+            queue = nc.sync if quad < 2 else nc.scalar
+            queue.dma_start(out_2[0, 4 * quad : 4 * quad + 4, :].bitcast(I32), y_scales[32 * quad : 32 * quad + 4, :].bitcast(I32))

@@ -26,8 +26,8 @@ ARENA_WORDS = 2 * 768 + 2 * 1280 + 2 * N + 2 * 2 * T + 16
 
 CHUNKS = ((0, 768, 768), (768, 1408, 1408), (1408, 2048, 1600))
 THIRD_CHUNKS = ((0, 768, 768), (768, 1408, 1408), (1408, 2048, 1536))
-LAST_CHUNKS = ((0, 768, 768), (768, 1280, 1280), (1280, 1664, 1280), (1664, 2048, 1792))
-VECTOR_BANKS = ((0, 3), (1, 0), (1, 1))
+LAST_CHUNKS = ((0, 576, 576), (576, 1088, 1088), (1088, 1600, 1600), (1600, 2048, 1696))
+VECTOR_BANKS = ((0, 2), (0, 3), (1, 0), (1, 1))
 EXP_RUNS = (((0, 2), (2, 4)), ((2, 4), (0, 1), (1, 2)))
 
 
@@ -163,7 +163,7 @@ def tile_list_gap_of_two_picks_pl_kernel(tc, xt, wa_words, wa_scales, wb_words, 
         load_pair(2, THIRD_CHUNKS[:1])
         woven00 = weave(picked0[0], 0, "woven0_0", J, True, on="raw2_0")
         load_pair(2, THIRD_CHUNKS, 1)
-        nc.vector.tensor_copy(wa[:], wa_raw[:].rearrange("p z (m t) -> p z t m", t=PACK))
+        nc.vector.tensor_copy(wa[:].rearrange("p z t (b i) -> p z b t i", i=4), wa_raw[:].rearrange("p z (b i t) -> p z b t i", i=4, t=PACK))
         for h in range(2):
             for w in range(2):
                 gather(picked1[w, h], 2, w, h * HALF, (h + 1) * HALF)
@@ -176,88 +176,64 @@ def tile_list_gap_of_two_picks_pl_kernel(tc, xt, wa_words, wa_scales, wb_words, 
 
         woven1 = {}
         operands = {}
-        gather(picked1[0, 0], 3, 0, 0, HALF)
-        woven1[0, 0] = weave(picked1[0, 0], 0, "woven1_00", HALF, True)
-        gather(picked1[1, 0], 3, 1, 0, HALF)
-        woven1[1, 0] = weave(picked1[1, 0], 1, "woven1_10", HALF, True)
-        gather(picked1[1, 1], 3, 1, HALF, J)
-        woven1[1, 1] = weave(picked1[1, 1], 1, "woven1_11", HALF, True)
-        gather(picked1[0, 1], 3, 0, HALF, J)
-        operands[0, 0] = quantise(woven1[0, 0], "x1_00", HALF)
-        operands[1, 0] = quantise(woven1[1, 0], "x1_10", HALF)
-        woven1[0, 1] = weave(picked1[0, 1], 0, "woven1_01", HALF, False, tag="woven1_10")
-        operands[1, 1] = quantise(woven1[1, 1], "x1_11", HALF)
-        operands[0, 1] = quantise(woven1[0, 1], "x1_01", HALF)
+        for h in range(2):
+            for w in (1, 0):
+                gather(picked1[w, h], 3, w, h * HALF, (h + 1) * HALF)
+                woven1[w, h] = weave(picked1[w, h], w, "woven1_%d%d" % (w, h), HALF, True)
+        for h in range(2):
+            for w in (1, 0):
+                operands[w, h] = quantise(woven1[w, h], "x1_%d%d" % (w, h), HALF)
 
-        gap = sb("gap", [P, 2, PACK, HALF], F32)
+        gap = {(h, t0): sb("gap%d%d" % (h, t0), [P, t1 - t0, HALF], F32) for h in range(2) for t0, t1 in EXP_RUNS[h]}
+        gap_of = {(h, t): gap[h, t0][:, t - t0, :] for h in range(2) for t0, t1 in EXP_RUNS[h] for t in range(t0, t1)}
         decay = sb("decay", [P, 2, PACK, HALF], F32)
         for h in range(2):
             for t in range(PACK):
-                multiply(h, t, 1, 0, operands[0, h], 0)
+                multiply(h, t, 1, 1, operands[1, h], 0)
             for t in range(PACK):
-                multiply(h, t, 1, 1, operands[1, h], 0, stop=True)
+                multiply(h, t, 1, 0, operands[0, h], 0, stop=True)
             for t in range(PACK):
                 if (h, t) in VECTOR_BANKS:
                     twice = sb("twice%d%d" % (h, t), [P, HALF], F32)
                     nc.vector.tensor_scalar(twice[:], banks[h, t][:], 0.0, 2.0, ALU.max, ALU.mult)
-                    nc.vector.scalar_tensor_tensor(gap[:, h, t, :], banks[h, t][:], -1.0, twice[:], ALU.mult, ALU.add)
+                    nc.vector.scalar_tensor_tensor(gap_of[h, t], banks[h, t][:], -1.0, twice[:], ALU.mult, ALU.add)
                 else:
-                    nc.scalar.activation(gap[:, h, t, :], banks[h, t][:], ACT.Abs)
+                    nc.scalar.activation(gap_of[h, t], banks[h, t][:], ACT.Abs)
             for t0, t1 in EXP_RUNS[h]:
-                nc.scalar.activation(decay[:, h, t0:t1, :], gap[:, h, t0:t1, :], ACT.Exp, scale=-1.0)
+                nc.scalar.activation(decay[:, h, t0:t1, :], gap[h, t0][:], ACT.Exp, scale=-1.0)
         scaled = sb("scaled", [P, 2, PACK, HALF], F32, tag="twice11")
-        for h in range(2):
-            for t in range(PACK):
-                nc.vector.tensor_scalar(scaled[:, h, t, :], gap[:, h, t, :], gain[:, t : t + 1], None, ALU.mult)
+        for h, t in [(0, 0), (1, 1), (0, 1), (0, 2), (0, 3), (1, 0), (1, 2), (1, 3)]:
+            nc.vector.tensor_scalar(scaled[:, h, t, :], gap_of[h, t], gain[:, t : t + 1], None, ALU.mult)
 
-        rest = sb("rest", [P, 4, PACK, QUARTER], F32, tag="gap")
-        for c in range(4):
-            h, s = divmod(c, 2)
-            nc.scalar.activation(rest[:, c, :, :], decay[:, h, :, s * QUARTER : (s + 1) * QUARTER], ACT.Ln, bias=1.0)
+        rest = sb("rest", [P, 2, PACK, HALF], F32, tag="gap11")
+        for h in range(2):
+            for t in (0, 2):
+                nc.scalar.activation(rest[:, h, t : t + 2, :], decay[:, h, t : t + 2, :], ACT.Ln, bias=1.0)
 
         y_rows = out_0.rearrange("(p t) j -> p t j", t=PACK)
         words_out = out_1[0].rearrange("p j r -> p (j r)").bitcast(I32)
         y_codes = sb("y_codes", [P, J], U32)
         y_scales = sb("y_scales", [P, J], U8)
         ys = [sb("y%d" % h, [P, PACK, HALF], F32) for h in range(2)]
-        rounded = [sb("rounded%d" % c, [P, PACK * QUARTER], BF16) for c in range(4)]
+        rounded = [sb("rounded%d" % h, [P, PACK * HALF], BF16) for h in range(2)]
 
-        def finish(c):
-            h, s = divmod(c, 2)
-            cols = slice(s * QUARTER, (s + 1) * QUARTER)
+        for h in range(2):
             for t in range(PACK):
-                nc.vector.scalar_tensor_tensor(ys[h][:, t, cols], rest[:, c, t, :], gain[:, t : t + 1], scaled[:, h, t, cols], ALU.mult, ALU.add)
-
-        def round_off(c, on_scalar):
-            h, s = divmod(c, 2)
-            dst = rounded[c][:].rearrange("p (b i t) -> p b t i", i=4, t=PACK)
-            src = ys[h][:, :, s * QUARTER : (s + 1) * QUARTER].rearrange("p t (b i) -> p b t i", i=4)
-            if on_scalar:
-                nc.scalar.activation(dst, src, ACT.Copy)
-            else:
-                nc.vector.tensor_copy(dst, src)
-
-        def planes(c):
-            cols = slice(c * QUARTER, (c + 1) * QUARTER)
-            nc.vector.quantize_mx(out=y_codes[:, cols].bitcast(FP8X4), scales=y_scales[:, cols], in_=rounded[c][:])
-
-        finish(0)
-        finish(1)
-        nc.sync.dma_start(y_rows[:, :, 0:HALF], ys[0][:])
-        round_off(0, True)
-        round_off(1, True)
-        finish(2)
-        nc.sync.dma_start(y_rows[:, :, HALF : HALF + QUARTER], ys[1][:, :, 0:QUARTER])
-        finish(3)
-        nc.sync.dma_start(y_rows[:, :, HALF + QUARTER : J], ys[1][:, :, QUARTER:HALF])
-        round_off(2, False)
-        round_off(3, False)
-        planes(0)
-        planes(1)
-        nc.sync.dma_start(words_out[:, 0:HALF], y_codes[:, 0:HALF].bitcast(I32))
-        planes(2)
-        planes(3)
-        nc.sync.dma_start(words_out[:, HALF:J], y_codes[:, HALF:J].bitcast(I32))
+                nc.vector.scalar_tensor_tensor(ys[h][:, t, :], rest[:, h, t, :], gain[:, t : t + 1], scaled[:, h, t, :], ALU.mult, ALU.add)
+                if t % 2 == 1:
+                    nc.sync.dma_start(y_rows[:, t - 1 : t + 1, h * HALF : (h + 1) * HALF], ys[h][:, t - 1 : t + 1, :])
+        for h in range(2):
+            for s in range(2):
+                dst = rounded[h][:, s * PACK * QUARTER : (s + 1) * PACK * QUARTER].rearrange("p (b i t) -> p b t i", i=4, t=PACK)
+                src = ys[h][:, :, s * QUARTER : (s + 1) * QUARTER].rearrange("p t (b i) -> p b t i", i=4)
+                if (h, s) != (1, 0):
+                    nc.scalar.activation(dst, src, ACT.Copy)
+                else:
+                    nc.vector.tensor_copy(dst, src)
+        for h in range(2):
+            cols = slice(h * HALF, (h + 1) * HALF)
+            nc.vector.quantize_mx(out=y_codes[:, cols].bitcast(FP8X4), scales=y_scales[:, cols], in_=rounded[h][:])
+            nc.sync.dma_start(words_out[:, cols], y_codes[:, cols].bitcast(I32))
         for quad in range(4):
             queue = nc.sync if quad < 2 else nc.scalar
             queue.dma_start(out_2[0, 4 * quad : 4 * quad + 4, :].bitcast(I32), y_scales[32 * quad : 32 * quad + 4, :].bitcast(I32))

@@ -22,11 +22,11 @@ K_PASS = P * PACK
 HALF = J // 2
 QUARTER = J // 4
 ALIGN = 64
-ARENA_WORDS = 2 * 768 + 2 * 1280 + 2 * N + 2 * 2 * T + 16
+ARENA_WORDS = 2 * T + 2 * N + 2 * 2 * T + 16
 
-CHUNKS = ((0, 768, 768), (768, 1408, 1408), (1408, 2048, 1600))
-THIRD_CHUNKS = ((0, 768, 768), (768, 1408, 1408), (1408, 2048, 1536))
-LAST_CHUNKS = ((0, 576, 576), (576, 1088, 1088), (1088, 1600, 1600), (1600, 2048, 1696))
+CHUNKS = ((0, 1024, 1024), (1024, 2048, 1408))
+THIRD_CHUNKS = CHUNKS
+LAST_CHUNKS = ((0, 1024, 1024), (1024, 1664, 1024), (1664, 2048, 1792))
 VECTOR_BANKS = ((0, 2), (0, 3), (1, 0), (1, 1))
 EXP_RUNS = (((0, 2), (2, 4)), ((2, 4), (0, 1), (1, 2)))
 
@@ -38,7 +38,7 @@ def tile_list_gap_of_two_picks_pl_kernel(tc, xt, wa_words, wa_scales, wb_words, 
         psum = ctx.enter_context(tc.psum_pool(name="psum", bufs=1))
         arena = ctx.enter_context(tc.tile_pool(name="arena", bufs=1))
         places = {}
-        first_free = [2 * 768 * 4]
+        first_free = [2 * 1024 * 4]
 
         def in_arena(name, shape, dtype, nbytes, on=None):
             if on is None:
@@ -167,7 +167,7 @@ def tile_list_gap_of_two_picks_pl_kernel(tc, xt, wa_words, wa_scales, wb_words, 
         for h in range(2):
             for w in range(2):
                 gather(picked1[w, h], 2, w, h * HALF, (h + 1) * HALF)
-        pass0[0] = quantise(woven00, "x0_0", J, on="raw2_2")
+        pass0[0] = quantise(woven00, "x0_0", J, on="raw2_1")
         load_pair(3, LAST_CHUNKS)
         for h in range(2):
             for t in range(PACK):

from contextlib import ExitStack

import concourse.mybir as mybir

K, T, J, N = 1024, 2048, 512, 512
FLOPS = 2 * 2 * K * N * J

F32 = mybir.dt.float32
BF16 = mybir.dt.bfloat16
I32 = mybir.dt.int32
U32 = mybir.dt.uint32
U16 = mybir.dt.uint16
U8 = mybir.dt.uint8
FP8X4 = mybir.dt.float8_e4m3fn_x4
FP4X4 = mybir.dt.float4_e2m1fn_x4
ALU = mybir.AluOpType
ACT = mybir.ActivationFunctionType

P = 128
PACK = 4
K_PASS = P * PACK
HALF = J // 2
QUARTER = J // 4
ALIGN = 64
ARENA_WORDS = 2 * T + 2 * N + 2 * 2 * T + 16

CHUNKS = ((0, 1024, 1024), (1024, 2048, 1408))
THIRD_CHUNKS = CHUNKS
LAST_CHUNKS = ((0, 1024, 1024), (1024, 1664, 1024), (1664, 2048, 1792))
VECTOR_BANKS = ((0, 2), (0, 3), (1, 0), (1, 1))
EXP_RUNS = (((0, 2), (2, 4)), ((2, 4), (0, 1), (1, 2)))


def tile_list_gap_of_two_picks_pl_kernel(tc, xt, wa_words, wa_scales, wb_words, wb_scales, gm, offs, offs2, out_0, out_1, out_2):
    nc = tc.nc
    with ExitStack() as ctx:
        keep = ctx.enter_context(tc.tile_pool(name="keep", bufs=1))
        psum = ctx.enter_context(tc.psum_pool(name="psum", bufs=1))
        arena = ctx.enter_context(tc.tile_pool(name="arena", bufs=1))
        places = {}
        first_free = [2 * 1024 * 4]

        def in_arena(name, shape, dtype, nbytes, on=None):
            if on is None:
                places[name] = first_free[0]
                first_free[0] = first_free[0] + (nbytes + ALIGN - 1) // ALIGN * ALIGN
            return arena.tile(shape, dtype, name=name, tag=name, align_bytes=ALIGN, offset=places[on or name])

        whole = arena.tile([P, ARENA_WORDS], F32, name="whole", align_bytes=ALIGN, offset=0)

        def sb(name, shape, dtype, tag=None):
            return keep.tile(shape, dtype, name=name, tag=tag or name, align_bytes=ALIGN)

        lists = [keep.tile([P, J // 16], U16, name="first_list"), keep.tile([P, J // 16], U16, name="second_list")]
        wa_raw = in_arena("wa_raw", [P, 2, N], I32, 8 * N)
        wb_raw = sb("wb_raw", [P, 2, 2 * N], U8)
        ws_raw = sb("ws_raw", [P, 2, N], U8)
        wa = sb("wa", [P, 2, PACK, P], I32)
        wb = sb("wb", [P, 2, PACK, 2 * P], U8)
        gain = in_arena("gain", [P, PACK], F32, 16)
        windows = [sb("window%d" % i, [P, 2 * T], BF16) for i in range(4)]
        banks = {(h, t): psum.tile([P, HALF], F32, name="bank%d%d" % (h, t)) for h in range(2) for t in range(PACK)}

        nc.gpsimd.memset(ws_raw[:].rearrange("p z n -> p (z n)").bitcast(U32), 0)

        small = [lambda: nc.sync.dma_start(lists[0][:], offs), lambda: nc.sync.dma_start(lists[1][:], offs2)]

        def scale_load(queue, src, row0, quad):
            dst = ws_raw[32 * quad + row0 : 32 * quad + row0 + 4, :, :].bitcast(I32)
            queue.dma_start(dst, src[:, 4 * quad : 4 * quad + 4, :].rearrange("z r n -> r z n").bitcast(I32))

        for quad in range(4):
            scale_load(nc.gpsimd, wb_scales, 0, quad)

        def load_pair(i, chunks, first=0):
            z, u = divmod(i, 2)
            rows = xt[z * K_PASS : (z + 1) * K_PASS, :].rearrange("(p u e) c -> p u e c", u=2, e=2)
            for n, (c0, c1, cut) in list(enumerate(chunks))[first:]:
                name = "raw%d_%d" % (i, n)
                if (i, n) == (0, 0):
                    raw = whole[:, : 2 * (c1 - c0)].rearrange("p (e c) -> p e c", e=2)
                elif (i, n) <= (1, 0):
                    raw = sb(name, [P, 2, c1 - c0], F32)[:]
                else:
                    raw = in_arena(name, [P, 2, c1 - c0], F32, 8 * (c1 - c0))[:]
                nc.sync.dma_start(raw, rows[:, u, :, c0:c1])
                if (i, n) == (1, 0):
                    for quad in range(4):
                        scale_load(nc.sync, wa_scales, 4, quad)
                if (i, n) == (2, 0):
                    nc.sync.dma_start(wa_raw[:], wa_words.rearrange("z p n r -> p z (n r)").bitcast(I32))
                if (i, n) == (2, 1):
                    nc.sync.dma_start(gain[:], gm.rearrange("(p t) o -> p (t o)", t=PACK))
                if i + n >= 1:
                    for job in small[:2]:
                        job()
                    small[:2] = []
                dst = windows[i][:].rearrange("p (c e) -> p c e", e=2)
                src = raw.rearrange("p e c -> p c e")
                if cut > c0:
                    nc.scalar.activation(dst[:, c0:cut, :], src[:, : cut - c0, :], ACT.Copy)
                if cut < c1:
                    nc.vector.tensor_copy(dst[:, cut:c1, :], src[:, cut - c0 :, :])

        def gather(picked, i, which, j0, j1):
            window = windows[i][:].bitcast(U32)
            nc.vector.tensor_copy(picked[:, i % 2, :], window.indirect(lists[which][:, j0 // 16 : j1 // 16]))

        def weave(picked, which, name, width, on_scalar, tag=None, on=None):
            woven = in_arena(name, [P, PACK * width], BF16, 0, on) if on else sb(name, [P, PACK * width], BF16, tag)
            if which == 0 and on_scalar:
                dst = woven[:].bitcast(U32).rearrange("p (j u) -> p j u", u=2)
                nc.scalar.copy(dst, picked[:].rearrange("p u j -> p j u"))
            elif which == 0:
                dst = woven[:].bitcast(I32).rearrange("p (j u) -> p j u", u=2)
                nc.vector.tensor_copy(dst, picked[:].bitcast(I32).rearrange("p u j -> p j u"))
            else:
                dst = woven[:].rearrange("p (j u e) -> p j u e", u=2, e=2)
                src = picked[:].bitcast(BF16).rearrange("p u (j e) -> p j u e", e=2)
                if on_scalar:
                    nc.scalar.activation(dst, src, ACT.Copy, scale=-1.0)
                else:
                    nc.vector.tensor_scalar(dst, src, -1.0, None, ALU.mult)
            return woven

        def quantise(woven, name, width, on=None):
            codes = in_arena(name + "_codes", [P, width], U32, 0, on) if on else sb(name + "_codes", [P, width], U32)
            scales = sb(name + "_scales", [P, width], U8)
            nc.vector.quantize_mx(out=codes[:].bitcast(FP8X4), scales=scales[:], in_=woven[:])
            return codes, scales

        def multiply(h, t, z, which, operand, j0, start=False, stop=False):
            codes, scales = operand
            if which == 0:
                nc.tensor.matmul_mx(
                    out=banks[h, t][:], lhsT=wa[:, z, t, :].bitcast(FP8X4), lhsT_scale=ws[4:P, z, t, :],
                    rhs=codes[:, j0 : j0 + HALF].bitcast(FP8X4), rhs_scale=scales[:, j0 : j0 + HALF],
                    start=start, stop=stop)
            else:
                for s in range(2):
                    cols = slice(j0 + s * QUARTER, j0 + (s + 1) * QUARTER)
                    nc.tensor.matmul_mx(
                        out=banks[h, t][:, s * QUARTER : (s + 1) * QUARTER], lhsT=wb[:, z, t, :].bitcast(FP4X4),
                        lhsT_scale=ws[:, z, t, :], rhs=codes[:, cols].bitcast(FP8X4), rhs_scale=scales[:, cols],
                        start=False, stop=stop and s == 1)

        ws = sb("ws", [P, 2, PACK, P], U8, "wb_raw")


        picked0 = [sb("picked0_%d" % w, [P, 2, J], U32) for w in range(2)]
        load_pair(0, CHUNKS)
        nc.sync.dma_start(wb_raw[:].bitcast(I32), wb_words.rearrange("z p c -> p z c").bitcast(I32))
        for w in range(2):
            gather(picked0[w], 0, w, 0, J)
        nc.vector.tensor_copy(wb[:].bitcast(U16), wb_raw[:].bitcast(U16).rearrange("p z (m t) -> p z t m", t=PACK))
        load_pair(1, CHUNKS)
        nc.vector.tensor_copy(ws[:], ws_raw[:].rearrange("p z (m t) -> p z t m", t=PACK))
        for w in range(2):
            gather(picked0[w], 1, w, 0, J)
        pass0 = {1: quantise(weave(picked0[1], 1, "woven0_1", J, False), "x0_1", J)}

        picked1 = {(w, h): sb("picked1_%d%d" % (w, h), [P, 2, HALF], U32) for w in range(2) for h in range(2)}
        load_pair(2, THIRD_CHUNKS[:1])
        woven00 = weave(picked0[0], 0, "woven0_0", J, True, on="raw2_0")
        load_pair(2, THIRD_CHUNKS, 1)
        nc.vector.tensor_copy(wa[:].rearrange("p z t (b i) -> p z b t i", i=4), wa_raw[:].rearrange("p z (b i t) -> p z b t i", i=4, t=PACK))
        for h in range(2):
            for w in range(2):
                gather(picked1[w, h], 2, w, h * HALF, (h + 1) * HALF)
        pass0[0] = quantise(woven00, "x0_0", J, on="raw2_1")
        load_pair(3, LAST_CHUNKS)
        for h in range(2):
            for t in range(PACK):
                multiply(h, t, 0, 0, pass0[0], h * HALF, start=True)
                multiply(h, t, 0, 1, pass0[1], h * HALF)

        woven1 = {}
        operands = {}
        for h in range(2):
            for w in (1, 0):
                gather(picked1[w, h], 3, w, h * HALF, (h + 1) * HALF)
                woven1[w, h] = weave(picked1[w, h], w, "woven1_%d%d" % (w, h), HALF, True)
        for h in range(2):
            for w in (1, 0):
                operands[w, h] = quantise(woven1[w, h], "x1_%d%d" % (w, h), HALF)

        gap = {(h, t0): sb("gap%d%d" % (h, t0), [P, t1 - t0, HALF], F32) for h in range(2) for t0, t1 in EXP_RUNS[h]}
        gap_of = {(h, t): gap[h, t0][:, t - t0, :] for h in range(2) for t0, t1 in EXP_RUNS[h] for t in range(t0, t1)}
        decay = sb("decay", [P, 2, PACK, HALF], F32)
        for h in range(2):
            for t in range(PACK):
                multiply(h, t, 1, 1, operands[1, h], 0)
            for t in range(PACK):
                multiply(h, t, 1, 0, operands[0, h], 0, stop=True)
            for t in range(PACK):
                if (h, t) in VECTOR_BANKS:
                    twice = sb("twice%d%d" % (h, t), [P, HALF], F32)
                    nc.vector.tensor_scalar(twice[:], banks[h, t][:], 0.0, 2.0, ALU.max, ALU.mult)
                    nc.vector.scalar_tensor_tensor(gap_of[h, t], banks[h, t][:], -1.0, twice[:], ALU.mult, ALU.add)
                else:
                    nc.scalar.activation(gap_of[h, t], banks[h, t][:], ACT.Abs)
            for t0, t1 in EXP_RUNS[h]:
                nc.scalar.activation(decay[:, h, t0:t1, :], gap[h, t0][:], ACT.Exp, scale=-1.0)
        scaled = sb("scaled", [P, 2, PACK, HALF], F32, tag="twice11")
        for h, t in [(0, 0), (1, 1), (0, 1), (0, 2), (0, 3), (1, 0), (1, 2), (1, 3)]:
            nc.vector.tensor_scalar(scaled[:, h, t, :], gap_of[h, t], gain[:, t : t + 1], None, ALU.mult)

        rest = sb("rest", [P, 2, PACK, HALF], F32, tag="gap11")
        for h in range(2):
            for t in (0, 2):
                nc.scalar.activation(rest[:, h, t : t + 2, :], decay[:, h, t : t + 2, :], ACT.Ln, bias=1.0)

        y_rows = out_0.rearrange("(p t) j -> p t j", t=PACK)
        words_out = out_1[0].rearrange("p j r -> p (j r)").bitcast(I32)
        y_codes = sb("y_codes", [P, J], U32)
        y_scales = sb("y_scales", [P, J], U8)
        ys = [sb("y%d" % h, [P, PACK, HALF], F32) for h in range(2)]
        rounded = [sb("rounded%d" % h, [P, PACK * HALF], BF16) for h in range(2)]

        for h in range(2):
            for t in range(PACK):
                nc.vector.scalar_tensor_tensor(ys[h][:, t, :], rest[:, h, t, :], gain[:, t : t + 1], scaled[:, h, t, :], ALU.mult, ALU.add)
                if t % 2 == 1:
                    nc.sync.dma_start(y_rows[:, t - 1 : t + 1, h * HALF : (h + 1) * HALF], ys[h][:, t - 1 : t + 1, :])
        for h in range(2):
            for s in range(2):
                dst = rounded[h][:, s * PACK * QUARTER : (s + 1) * PACK * QUARTER].rearrange("p (b i t) -> p b t i", i=4, t=PACK)
                src = ys[h][:, :, s * QUARTER : (s + 1) * QUARTER].rearrange("p t (b i) -> p b t i", i=4)
                if (h, s) != (1, 0):
                    nc.scalar.activation(dst, src, ACT.Copy)
                else:
                    nc.vector.tensor_copy(dst, src)
        for h in range(2):
            cols = slice(h * HALF, (h + 1) * HALF)
            nc.vector.quantize_mx(out=y_codes[:, cols].bitcast(FP8X4), scales=y_scales[:, cols], in_=rounded[h][:])
            nc.sync.dma_start(words_out[:, cols], y_codes[:, cols].bitcast(I32))
        for quad in range(4):
            queue = nc.sync if quad < 2 else nc.scalar
            queue.dma_start(out_2[0, 4 * quad : 4 * quad + 4, :].bitcast(I32), y_scales[32 * quad : 32 * quad + 4, :].bitcast(I32))
